import numpy as np
import ml_dtypes


def mxq(x, axis, fmt="e4m3"):
    dtype, down = {"e4m3": (ml_dtypes.float8_e4m3fn, 7), "e5m2": (ml_dtypes.float8_e5m2, 14)}[fmt]
    v = np.moveaxis(np.asarray(x, np.float32).astype(ml_dtypes.bfloat16).astype(np.float64), axis, -1)
    blocks = v.reshape(v.shape[:-1] + (-1, 32))
    amax = np.abs(blocks).max(-1, keepdims=True)
    byte = np.maximum(np.where(amax > 0, np.frexp(amax)[1] - 1 + 127, 0) - down, 1)
    scale = np.exp2(byte - 127.0)
    codes = (blocks / scale).astype(np.float32).astype(dtype).astype(np.float64)
    return np.moveaxis((codes * scale).reshape(v.shape), -1, axis)


WIDE = False


def mx_kscale(k):
    if not WIDE:
        return np.ones(k)
    levels = np.array([10, -10, 5, -5, 0])
    if k % 512:
        return np.exp2(np.random.permutation(np.resize(levels, k // 32))).repeat(32)
    a = np.empty((k // 512, 16))
    for p in range(k // 512):
        a[p, :8] = np.random.permutation(np.resize(levels, 8))
        for g in range(8):
            far = levels[np.abs(levels - a[p, g]) >= 10]
            a[p, g + 8] = far[np.random.randint(len(far))]
    return np.exp2(a.ravel()).repeat(32)


def f64(x):
    return np.asarray(x).astype(np.float64)


def striped(idx):
    return np.tile(idx.reshape(-1, 16).T, (8, 1)).astype(np.uint16)


def unstriped(offs):
    return offs[:16].T.reshape(-1).astype(np.int64)


E2M1 = np.array([0.0, 0.5, 1.0, 1.5, 2.0, 3.0, 4.0, 6.0, -0.0, -0.5, -1.0, -1.5, -2.0, -3.0, -4.0, -6.0])


def pack_weight(w, fmt):
    k, n = w.shape
    w = f64(np.asarray(w, np.float32).astype(ml_dtypes.bfloat16)).reshape(k // 32, 32, n)
    amax = np.abs(w).max(1)
    if fmt == "e4m3":
        byte = np.frexp(amax)[1] - 1 + 127 - 7
    else:
        mant, ex = np.frexp(amax / 6.0)
        byte = np.where(mant > 0.5, ex, ex - 1) + 127
    byte = np.clip(np.where(amax > 0, byte, 1), 1, 254)
    scaled = (w * np.exp2(127.0 - byte)[:, None, :]).reshape(k, n).astype(np.float32)
    by_word = np.ascontiguousarray(scaled.reshape(k // 512, 128, 4, n).transpose(0, 1, 3, 2))
    if fmt == "e4m3":
        words = by_word.astype(ml_dtypes.float8_e4m3fn).view(np.uint8)
    else:
        c = by_word.astype(ml_dtypes.float4_e2m1fn).view(np.uint8) & 0xF
        words = (c[..., 0::2] | (c[..., 1::2] << 4)).reshape(k // 512, 128, 2 * n)
    return np.ascontiguousarray(words), np.ascontiguousarray(byte.astype(np.uint8).reshape(k // 512, 16, n))


def unpack_weight(words, scales, fmt):
    g, _, n = scales.shape
    words = np.ascontiguousarray(words).reshape(g, 128, n, -1)
    if fmt == "e4m3":
        vals = words.view(ml_dtypes.float8_e4m3fn).astype(np.float64)
    else:
        nib = np.empty((g, 128, n, 4), np.uint8)
        nib[..., 0::2] = words & 0xF
        nib[..., 1::2] = words >> 4
        vals = E2M1[nib]
    vals = vals * np.repeat(np.exp2(scales.astype(np.float64) - 127.0), 8, axis=1)[..., None]
    return vals.transpose(0, 1, 3, 2).reshape(g * 512, n)


def gelu(v):
    return 0.5 * v * (1.0 + np.tanh(np.sqrt(2.0 / np.pi) * (v + 0.044715 * v**3)))


def bf(x):
    return np.asarray(x, np.float32).astype(ml_dtypes.bfloat16)


def planes(Y):
    n, m = Y.shape
    b = f64(bf(Y)).reshape(n // 32, 32, m)
    amax = np.abs(b).max(1)
    byte = np.clip(np.where(amax > 0, np.frexp(amax)[1] - 1 + 127 - 7, 1), 1, 254)
    codes = (b * np.exp2(127.0 - byte)[:, None, :]).reshape(n, m).astype(np.float32).astype(ml_dtypes.float8_e4m3fn).view(np.uint8)
    words = codes.reshape(n // 512, 128, 4, m).transpose(0, 1, 3, 2)
    return np.ascontiguousarray(words), np.ascontiguousarray(byte.astype(np.uint8).reshape(n // 512, 16, m))


K, T, S, T3, P, H, N = 512, 4096, 1024, 2048, 512, 1024, 1024

def setup_inputs():
    n = np.random.standard_normal
    s = mx_kscale(K)[:, None]
    u = mx_kscale(H)[:, None]
    d = {}
    d["tab_words"], d["tab_scales"] = pack_weight(n((K, T)) * s, "e4m3")
    d["offs"] = striped(np.random.permutation(T)[:S])
    d["tab2_words"], d["tab2_scales"] = pack_weight(n((K, T3)) * s, "e4m3")
    d["offs2"] = striped(np.random.permutation(T3)[:P])
    d["pos1"] = striped(np.random.permutation(S)[:P])
    d["w1"] = (n((K, H)) / K ** 0.5 / s * u.T).astype(np.float32)
    d["terrain"] = np.exp(0.5 * n((H, S))).astype(np.float32)
    d["w2_words"], d["w2_scales"] = pack_weight(n((K, H)) / K ** 0.5 / s * u.T, "e2m1")
    d["bias"] = (0.7 * n(H) * u[:, 0]).astype(np.float32)
    d["wgs"] = np.exp(0.3 * n((128, P))).astype(np.float32)
    d["w3_words"], d["w3_scales"] = pack_weight(1.2 * n((H, H)) / H ** 0.5 / u, "e4m3")
    d["gain"] = (1.2 * np.exp(0.3 * n(H)) * u[:, 0]).astype(np.float32)
    d["w4"] = (0.6 * n((H, N)) / H ** 0.5 / u * np.exp(0.8 * n(N))[None, :]).astype(np.float32)
    return d

def reference(tab_words, tab_scales, offs, tab2_words, tab2_scales, offs2, pos1, w1, terrain,
              w2_words, w2_scales, bias, wgs, w3_words, w3_scales, gain, w4):
    v = unpack_weight(tab_words, tab_scales, "e4m3")[:, unstriped(offs)]
    v2 = unpack_weight(tab2_words, tab2_scales, "e4m3")[:, unstriped(offs2)]
    w2 = unpack_weight(w2_words, w2_scales, "e2m1")
    w3 = unpack_weight(w3_words, w3_scales, "e4m3")
    a = (mxq(f64(w1), 0, "e4m3").T @ v) * f64(terrain)
    b = (w2.T @ v2) + f64(bias)[:, None]
    placed = np.zeros((H, S))
    placed[:, unstriped(pos1)] = np.tile(f64(wgs), (H // 128, 1)) * b
    z = a - placed
    x = f64(gain)[:, None] * np.tanh(w3.T @ mxq(z, 0, "e4m3")) + a
    y = mxq(f64(w4), 0, "e4m3").T @ mxq(x, 0, "e4m3")
    words, scales = planes(y)
    return y, words, scales

@@ -1,0 +1,414 @@
+from contextlib import ExitStack
+
+import concourse.mybir as mybir
+from concourse.masks import make_identity
+
+K, T, S, T2, L, H, N = 512, 4096, 1024, 2048, 512, 1024, 1024
+FLOPS = 2 * (K * H * S + K * H * L + H * H * S + H * N * S)
+
+F32 = mybir.dt.float32
+BF16 = mybir.dt.bfloat16
+I32 = mybir.dt.int32
+U32 = mybir.dt.uint32
+U16 = mybir.dt.uint16
+U8 = mybir.dt.uint8
+FP8X4 = mybir.dt.float8_e4m3fn_x4
+FP4X4 = mybir.dt.float4_e2m1fn_x4
+MULT = mybir.AluOpType.mult
+ADD = mybir.AluOpType.add
+ACT = mybir.ActivationFunctionType
+
+P = 128
+PACK = 4
+GROUP = P * PACK
+GROUPS = H // GROUP
+BANK = 512
+HALF = 512
+CHUNK_WIDTHS = (256, 256, 256, 256)
+CHUNKS = [(sum(CHUNK_WIDTHS[:c]), width) for c, width in enumerate(CHUNK_WIDTHS)]
+ALIGN = 64
+KIB = 1024
+ROOMS = {
+    "w1_raw0": 0, "w4_raw01": 0, "track10": 0,
+    "wgs_rows": 7,
+    "w1_raw1": 8, "track11": 8, "w4_raw11": 12, "w3_raw": 16,
+    "w4_raw00": 24, "track00": 24,
+    "w2_raw": 31,
+    "w4_raw10": 32, "track01": 32,
+    "tab2_all": 40, "tab_all": 40, "squashed": 40, "x_planar": 52,
+    "w2_plane": 56, "page3": 56,
+    "rumen0": 60, "page4": 60, "rumen1": 64, "page5": 64, "rumen2": 68, "page6": 68, "rumen3": 72, "page7": 72,
+    "w1_codes0": 76, "rumen5": 76, "w1_plane0": 78, "rumen6": 78,
+    "v_codes0": 80, "rumen7": 80, "w4_codes": 80,
+    "minus_wgs3": 88, "w3_codes": 88,
+    "w1_rounded": 96, "z_pairs": 96,
+    "spread": 104, "tab_plane": 104, "z_rounded": 104,
+    "tab2_plane": 108, "w3_plane": 108,
+}
+
+
+def tile_list_reindeer_route_features_kernel(
+    tc, tab_words, tab_scales, offs, tab2_words, tab2_scales, offs2, pos1, w1, terrain,
+    w2_words, w2_scales, bias, wgs, w3_words, w3_scales, gain, w4, out_0, out_1, out_2,
+):
+    nc = tc.nc
+
+    def load_scale_rows(queues, plane, scales):
+        passes = scales.shape[0]
+        for q, queue in enumerate(queues):
+            queue.dma_start(
+                out=plane[32 * q : 32 * q + 4 * passes, :].bitcast(I32),
+                in_=scales[:, 4 * q : 4 * q + 4, :].bitcast(I32),
+            )
+
+    def packed_words(words):
+        return words.rearrange("p c i -> p (c i)").bitcast(I32)
+
+    with ExitStack() as ctx:
+        lists = ctx.enter_context(tc.tile_pool(name="lists", bufs=1))
+        keep = ctx.enter_context(tc.tile_pool(name="keep", bufs=1))
+        turns = ctx.enter_context(tc.tile_pool(name="turns", bufs=1))
+        psum = ctx.enter_context(tc.psum_pool(name="psum", bufs=1))
+
+        def sbuf(name, shape, dtype, bufs=1):
+            if name in ROOMS:
+                return turns.tile(shape, dtype, name=name, tag=name, bufs=bufs, align_bytes=ALIGN,
+                                  offset=ROOMS[name] * KIB)
+            return keep.tile(shape, dtype, name=name, tag=name, bufs=bufs, align_bytes=ALIGN)
+
+        def bank(tag, shape):
+            return psum.tile(shape, F32, name=tag, tag=tag, bufs={"sums": 3, "turn": 3, "outer": 2}[tag])
+
+        idx2 = lists.tile([P, L // 16], U16, name="idx2")
+        place = lists.tile([P, L // 16], U16, name="place")
+        idx = lists.tile([P, S // 16], U16, name="idx")
+
+        tab2_plane = sbuf("tab2_plane", [P, T2], U8)
+        w2_plane = sbuf("w2_plane", [P, H], U8)
+        for plane in (tab2_plane, w2_plane):
+            nc.vector.memset(plane[:].bitcast(I32), 0)
+        identity = sbuf("identity", [P, P], F32)
+        make_identity(nc, identity[:])
+        warm = sbuf("warm", [P, 1], F32)
+        nc.scalar.activation(out=warm[:], in_=identity[:, 0:1], func=ACT.Tanh)
+
+        slots = [(g, t) for g in range(GROUPS) for t in range(PACK)]
+
+        wgs_rows = sbuf("wgs_rows", [P, L], F32)
+        w2_raw = sbuf("w2_raw", [P, 2 * H], U8)
+        tab2_all = sbuf("tab2_all", [P, T2], U32)
+        bias_col = sbuf("bias_col", [P, GROUPS, PACK], F32)
+        gain_col = sbuf("gain_col", [P, GROUPS, PACK], F32)
+
+        nc.sync.dma_start(idx2[:], offs2)
+        nc.sync.dma_start(out=bias_col[:], in_=bias.rearrange("(g p t) -> p g t", p=P, t=PACK))
+        nc.sync.dma_start(place[:], pos1)
+        nc.sync.dma_start(idx[:], offs)
+        nc.sync.dma_start(out=wgs_rows[:], in_=wgs)
+        nc.sync.dma_start(out=w2_raw[:].bitcast(I32), in_=w2_words[0].bitcast(I32))
+        nc.sync.dma_start(out=gain_col[:], in_=gain.rearrange("(g p t) -> p g t", p=P, t=PACK))
+        nc.sync.dma_start(out=tab2_all[:].bitcast(I32), in_=packed_words(tab2_words[0]))
+        load_scale_rows([nc.sync] * 4, tab2_plane, tab2_scales)
+        load_scale_rows([nc.sync] * 4, w2_plane, w2_scales)
+
+        def load_weight(name, weight_rows, g):
+            raw = sbuf(name, [P, PACK, GROUP], F32)
+            nc.sync.dma_start(
+                out=raw[:],
+                in_=weight_rows[:, g * GROUP : (g + 1) * GROUP].rearrange("(p j) c -> p j c", j=PACK),
+            )
+            return raw
+
+        turned = bank("turn", [P, L // P, P])
+        for jb in range(L // P):
+            nc.tensor.transpose(turned[:, jb, :], wgs_rows[:, jb * P : (jb + 1) * P], identity[:])
+        minus_wgs = []
+        for t in range(PACK):
+            spread = sbuf("spread", [P, L // P, 4, 32], F32, bufs=2)
+            nc.scalar.activation(
+                out=spread[:],
+                in_=turned[:].rearrange("j b (c t) -> j b t c", t=PACK)[:, :, t : t + 1, :].to_broadcast(
+                    [P, L // P, 4, 32]),
+                func=ACT.Copy, scale=-1.0,
+            )
+            back = bank("turn", [P, L // P, P])
+            for jb in range(L // P):
+                nc.tensor.transpose(back[:, jb, :], spread[:, jb, :, :].rearrange("j q c -> j (q c)"), identity[:])
+            minus_wgs.append(sbuf("minus_wgs%d" % t, [P, L], F32))
+            nc.scalar.copy(out=minus_wgs[t][:], in_=back[:].rearrange("p b j -> p (b j)"))
+
+        w2_codes = sbuf("w2_codes", [P, 2 * H], U8)
+        w2_dealt_plane = sbuf("w2_dealt_plane", [P, H], U8)
+        nc.vector.tensor_copy(
+            out=w2_codes[:].rearrange("p (g t m b) -> p g m t b", g=GROUPS, t=PACK, b=2),
+            in_=w2_raw[:].rearrange("p (g m t b) -> p g m t b", g=GROUPS, t=PACK, b=2),
+        )
+        nc.vector.tensor_copy(
+            out=w2_dealt_plane[:].rearrange("p (g t m) -> p g m t", g=GROUPS, t=PACK),
+            in_=w2_plane[:].rearrange("p (g m t) -> p g m t", g=GROUPS, t=PACK),
+        )
+
+        v2_plane = sbuf("v2_plane", [P, L], U8)
+        v2_codes = sbuf("v2_codes", [P, L], U32)
+        nc.vector.tensor_copy(v2_plane[:], tab2_plane[:].indirect(idx2[:]))
+        nc.vector.tensor_copy(v2_codes[:], tab2_all[:].indirect(idx2[:]))
+
+        pages = {}
+
+        def clear_page(s, engine):
+            pages[s] = sbuf("page%d" % s, [P, S], F32)
+            engine.memset(pages[s][:], 0.0)
+
+        for s in range(3):
+            clear_page(s, nc.vector)
+        clear_page(3, nc.gpsimd)
+
+        def load_w4(a, g):
+            return load_weight("w4_raw%d%d" % (a, g), w4[a * GROUP : (a + 1) * GROUP, :], g)
+
+        w1_raw = [load_weight("w1_raw%d" % g, w1, g) for g in range(GROUPS)]
+        w4_raw = {(a, 0): load_w4(a, 0) for a in range(GROUPS)}
+        tab_all = sbuf("tab_all", [P, T], U32)
+        nc.sync.dma_start(out=tab_all[:].bitcast(I32), in_=packed_words(tab_words[0]))
+        tab_plane = sbuf("tab_plane", [P, T], U8)
+        nc.gpsimd.memset(tab_plane[:].bitcast(I32), 0)
+        load_scale_rows([nc.sync] * 4, tab_plane, tab_scales)
+
+        def place_rumen(s):
+            g, t = slots[s]
+            sums = bank("outer", [P, L])
+            nc.tensor.matmul_mx(
+                out=sums[:],
+                lhsT=w2_codes[:, 2 * P * s : 2 * P * (s + 1)].bitcast(FP4X4),
+                lhsT_scale=w2_dealt_plane[:, P * s : P * (s + 1)],
+                rhs=v2_codes[:].bitcast(FP8X4), rhs_scale=v2_plane[:], start=True, stop=True,
+            )
+            rumen = sbuf("rumen%d" % s, [P, L], F32)
+            nc.scalar.activation(out=rumen[:], in_=sums[:], func=ACT.Identity, bias=bias_col[:, g, t : t + 1])
+            nc.vector.tensor_tensor(pages[s][:].indirect(place[:]), rumen[:], minus_wgs[t][:], MULT)
+
+        for s in range(5):
+            place_rumen(s)
+            if s < 4:
+                clear_page(s + 4, nc.gpsimd)
+
+        def round_weight(raw, rounded):
+            nc.scalar.copy(
+                out=rounded[:].rearrange("p (t m) j -> p m j t", t=PACK),
+                in_=raw[:].rearrange("p j (m t) -> p m j t", t=PACK),
+            )
+
+        w1_mx = []
+        for g in range(GROUPS):
+            rounded = sbuf("w1_rounded", [P, GROUP, PACK], BF16, bufs=2)
+            round_weight(w1_raw[g], rounded)
+            codes = sbuf("w1_codes%d" % g, [P, GROUP], U32)
+            plane = sbuf("w1_plane%d" % g, [P, GROUP], U8)
+            nc.vector.quantize_mx(out=codes[:].bitcast(FP8X4), scales=plane[:],
+                                  in_=rounded[:].rearrange("p c j -> p (c j)"))
+            w1_mx.append((codes, plane))
+
+        v_mx = []
+        for h in range(S // HALF):
+            picked = idx[:, h * HALF // 16 : (h + 1) * HALF // 16]
+            codes = sbuf("v_codes%d" % h, [P, HALF], U32)
+            plane = sbuf("v_plane%d" % h, [P, HALF], U8)
+            nc.vector.tensor_copy(plane[:], tab_plane[:].indirect(picked))
+            nc.vector.tensor_copy(codes[:], tab_all[:].indirect(picked))
+            v_mx.append((codes, plane))
+
+        w4_rounded = {}
+
+        def round_w4(g):
+            for a in range(GROUPS):
+                w4_rounded[a, g] = sbuf("w4_rounded%d%d" % (a, g), [P, GROUP, PACK], BF16)
+                round_weight(w4_raw[a, g], w4_rounded[a, g])
+
+        for a in range(GROUPS):
+            w4_raw[a, 1] = load_w4(a, 1)
+        round_w4(0)
+        track = {}
+        for g in range(GROUPS):
+            for h in range(S // HALF):
+                track[g, h] = sbuf("track%d%d" % (g, h), [P, PACK, HALF], F32)
+                nc.sync.dma_start(
+                    out=track[g, h][:],
+                    in_=terrain[g * GROUP : (g + 1) * GROUP, h * HALF : (h + 1) * HALF].rearrange(
+                        "(p t) j -> p t j", t=PACK),
+                )
+        round_w4(1)
+
+        w3_raw = sbuf("w3_raw", [P, GROUPS, H], U32)
+        w3_plane = sbuf("w3_plane", [P, H], U8)
+        nc.gpsimd.memset(w3_plane[:].bitcast(I32), 0)
+        for a in range(GROUPS):
+            nc.sync.dma_start(out=w3_raw[:, a, :].bitcast(I32), in_=packed_words(w3_words[a]))
+        load_scale_rows([nc.sync] * 4, w3_plane, w3_scales)
+
+        def track_features(g, h):
+            for t in range(PACK):
+                sums = bank("sums", [P, HALF])
+                nc.tensor.matmul_mx(
+                    out=sums[:],
+                    lhsT=w1_mx[g][0][:, t * P : (t + 1) * P].bitcast(FP8X4),
+                    lhsT_scale=w1_mx[g][1][:, t * P : (t + 1) * P],
+                    rhs=v_mx[h][0][:].bitcast(FP8X4), rhs_scale=v_mx[h][1][:], start=True, stop=True,
+                )
+                nc.vector.tensor_tensor(track[g, h][:, t, :], sums[:], track[g, h][:, t, :], MULT)
+
+        def track_columns(g, t, first, count):
+            h, inside = divmod(first, HALF)
+            return track[g, h][:, t, inside : inside + count]
+
+        def quantise(rounded, width, name, bufs):
+            codes = sbuf(name + "_codes", [P, width], U32, bufs=bufs)
+            plane = sbuf(name + "_plane", [P, width], U8, bufs=bufs)
+            nc.vector.quantize_mx(out=codes[:].bitcast(FP8X4), scales=plane[:], in_=rounded)
+            return codes, plane
+
+        def turned_pairs(g, u, c):
+            first, width = CHUNKS[c]
+            blocks = width // P
+            turned = bank("turn", [P, blocks, 2, P])
+            terms = []
+            for source in ("track", "page"):
+                for b in range(blocks):
+                    for e in range(2):
+                        t, start = 2 * u + e, first + b * P
+                        if source == "track":
+                            terms.append((turned[:, b, e, :], track_columns(g, t, start, P)))
+                        else:
+                            terms.append((turned[:, b, e, :], pages[PACK * g + t][:, start : start + P]))
+            for i, (out, term) in enumerate(terms):
+                nc.tensor.matmul(out, lhsT=term, rhs=identity[:], is_transpose=True,
+                                 start=(i == 0), stop=(i == len(terms) - 1))
+            pairs = sbuf("z_pairs", [P, blocks, P, 2], BF16, bufs=6)
+            nc.scalar.copy(out=pairs[:], in_=turned[:].rearrange("j b e p -> j b p e"))
+            return pairs
+
+        def difference(c, pairs):
+            width = CHUNKS[c][1]
+            blocks = width // P
+            back = bank("turn", [P, blocks, 2, P])
+            for b in range(blocks):
+                for u in range(2):
+                    words = pairs[u][:, b, :, :].rearrange("j p e -> j (p e)").bitcast(F32)
+                    nc.tensor.transpose(back[:, b, u, :], words, identity[:])
+            rounded = sbuf("z_rounded", [P, width * PACK], BF16, bufs=2)
+            nc.scalar.copy(
+                out=rounded[:].bitcast(F32).rearrange("p (b j u) -> p b j u", b=blocks, u=2),
+                in_=back[:].rearrange("p b u j -> p b j u"),
+            )
+            return quantise(rounded[:], width, "z", GROUPS * len(CHUNKS))
+
+        z_mx = {}
+        for h in range(S // HALF):
+            track_features(0, h)
+        place_rumen(5)
+        place_rumen(6)
+        for c in range(len(CHUNKS)):
+            z_mx[0, c] = difference(c, [turned_pairs(0, u, c) for u in range(2)])
+        track_features(1, 0)
+        place_rumen(7)
+        low_pairs = {c: turned_pairs(1, 0, c) for c in range(2)}
+
+        w3_codes = sbuf("w3_codes", [P, GROUPS, H], U32)
+        w3_dealt_plane = sbuf("w3_dealt_plane", [P, H], U8)
+        nc.vector.tensor_copy(
+            out=w3_codes[:].bitcast(I32).rearrange("p a (g t m) -> p (a g) m t", g=GROUPS, t=PACK),
+            in_=w3_raw[:].bitcast(I32).rearrange("p a (g m t) -> p (a g) m t", g=GROUPS, t=PACK),
+        )
+        nc.vector.tensor_copy(
+            out=w3_dealt_plane[:].rearrange("p (g t m) -> p g m t", g=GROUPS, t=PACK),
+            in_=w3_plane[:].rearrange("p (g m t) -> p g m t", g=GROUPS, t=PACK),
+        )
+
+        def interleave(copy, out, in_):
+            copy(
+                out=out.rearrange("p (c i t) -> p c t i", i=4, t=PACK),
+                in_=in_.rearrange("p t (c i) -> p c t i", i=4),
+            )
+
+        y_plane = sbuf("y_plane", [P, GROUPS, S], U8)
+
+        def products(tag, g, width, weights, moving, empty):
+            per_bank = BANK // width
+            for first_slot in range(0, PACK, per_bank):
+                sums = bank(tag, [P, per_bank, width])
+                for e in range(per_bank):
+                    for a in range(GROUPS):
+                        codes, plane = weights(a, g, first_slot + e)
+                        nc.tensor.matmul_mx(
+                            out=sums[:, e, :], lhsT=codes.bitcast(FP8X4), lhsT_scale=plane,
+                            rhs=moving[a][0][:].bitcast(FP8X4), rhs_scale=moving[a][1][:],
+                            start=(a == 0), stop=(a == GROUPS - 1),
+                        )
+                empty(slice(first_slot, first_slot + per_bank), sums[:])
+
+        def w3_slot(a, g, t):
+            cols = slice((PACK * g + t) * P, (PACK * g + t + 1) * P)
+            return w3_codes[:, a, cols], w3_dealt_plane[4 * a : P, cols]
+
+        def w4_slot(a, g, t):
+            cols = slice(t * P, (t + 1) * P)
+            return w4_codes[:, GROUPS * a + g, cols], w4_plane[:, GROUPS * a + g, cols]
+
+        def bounded(g, c):
+            first, width = CHUNKS[c]
+            squashed = sbuf("squashed", [P, PACK, width], F32, bufs=3)
+            products("sums", g, width, w3_slot, [z_mx[a, c] for a in range(GROUPS)],
+                     lambda held, sums: nc.scalar.activation(out=squashed[:, held, :], in_=sums, func=ACT.Tanh))
+            planar = sbuf("x_planar", [P, PACK, width], BF16, bufs=2)
+            for t in range(PACK):
+                nc.vector.scalar_tensor_tensor(
+                    out=planar[:, t, :], in0=squashed[:, t, :], scalar=gain_col[:, g, t : t + 1],
+                    in1=track_columns(g, t, first, width), op0=MULT, op1=ADD,
+                )
+            rounded = sbuf("x_rounded", [P, width * PACK], BF16, bufs=2)
+            interleave(nc.vector.tensor_copy, rounded[:], planar[:])
+            return quantise(rounded[:], width, "x", 4)
+
+        def result(g, c, x_mx):
+            first, width = CHUNKS[c]
+            cols = slice(first, first + width)
+            y = sbuf("y", [P, PACK, width], F32, bufs=3)
+            products("outer", g, width, w4_slot, x_mx,
+                     lambda held, sums: nc.scalar.copy(out=y[:, held, :], in_=sums))
+            nc.sync.dma_start(
+                out=out_0[g * GROUP : (g + 1) * GROUP, cols].rearrange("(p t) j -> p t j", t=PACK), in_=y[:])
+            rounded = sbuf("y_rounded", [P, width * PACK], BF16, bufs=2)
+            interleave(nc.vector.tensor_copy, rounded[:], y[:])
+            codes = sbuf("y_codes", [P, width], U32, bufs=3)
+            nc.vector.quantize_mx(out=codes[:].bitcast(FP8X4), scales=y_plane[:, g, cols], in_=rounded[:])
+            nc.sync.dma_start(out=packed_words(out_1[g])[:, cols], in_=codes[:].bitcast(I32))
+
+        def store_scale_rows(cols):
+            for q in range(4):
+                nc.sync.dma_start(
+                    out=out_2[:, 4 * q : 4 * q + 4, cols].rearrange("g r j -> r g j").bitcast(I32),
+                    in_=y_plane[32 * q : 32 * q + 4, :, cols].bitcast(I32),
+                )
+
+        w4_codes = sbuf("w4_codes", [P, GROUPS * GROUPS, GROUP], U32)
+        w4_plane = sbuf("w4_plane", [P, GROUPS * GROUPS, GROUP], U8)
+
+        x_mx = {}
+        for step in range(len(CHUNKS) + 2):
+            if step < len(CHUNKS):
+                low = low_pairs[step] if step in low_pairs else turned_pairs(1, 0, step)
+                z_mx[1, step] = difference(step, [low, turned_pairs(1, 1, step)])
+            if 1 <= step <= len(CHUNKS):
+                x_mx[step - 1] = [bounded(g, step - 1) for g in range(GROUPS)]
+            if step >= 2:
+                for g in range(GROUPS):
+                    result(g, step - 2, x_mx[step - 2])
+            if step == len(CHUNKS):
+                store_scale_rows(slice(0, CHUNKS[-1][0]))
+            if step == 0:
+                track_features(1, 1)
+                for (a, g), rounded in w4_rounded.items():
+                    nc.vector.quantize_mx(
+                        out=w4_codes[:, GROUPS * a + g, :].bitcast(FP8X4), scales=w4_plane[:, GROUPS * a + g, :],
+                        in_=rounded[:].rearrange("p c j -> p (c j)"))
+
+        store_scale_rows(slice(CHUNKS[-1][0], S))

@@ -30,20 +30,17 @@ ALIGN = 64
 KIB = 1024
 ROOMS = {
     "w1_raw0": 0, "w4_raw01": 0, "track10": 0,
-    "wgs_rows": 7,
+    "w2_raw": 7,
     "w1_raw1": 8, "track11": 8, "w4_raw11": 12, "w3_raw": 16,
     "w4_raw00": 24, "track00": 24,
-    "w2_raw": 31,
+    "tab2_plane": 31,
     "w4_raw10": 32, "track01": 32,
     "tab2_all": 40, "tab_all": 40, "squashed": 40, "x_planar": 52,
-    "w2_plane": 56, "page3": 56,
-    "rumen0": 60, "page4": 60, "rumen1": 64, "page5": 64, "rumen2": 68, "page6": 68, "rumen3": 72, "page7": 72,
-    "w1_codes0": 76, "rumen5": 76, "w1_plane0": 78, "rumen6": 78,
-    "v_codes0": 80, "rumen7": 80, "w4_codes": 80,
-    "minus_wgs3": 88, "w3_codes": 88,
-    "w1_rounded": 96, "z_pairs": 96,
-    "spread": 104, "tab_plane": 104, "z_rounded": 104,
-    "tab2_plane": 108, "w3_plane": 108,
+    "w1_codes0": 56, "rumen5": 56, "w1_plane0": 58, "rumen6": 58,
+    "v_codes0": 60, "rumen7": 60, "w4_codes": 60,
+    "minus_wgs3": 68, "w3_codes": 68,
+    "w1_rounded": 76, "z_pairs": 76,
+    "spread": 84, "tab_plane": 84, "z_rounded": 84,
 }
 
 
@@ -63,6 +60,12 @@ def tile_list_reindeer_route_features_kernel(
 
     def packed_words(words):
         return words.rearrange("p c i -> p (c i)").bitcast(I32)
+
+    def deal_columns(out, in_, run):
+        nc.vector.tensor_copy(
+            out=out.rearrange("p (g t c i) -> p g c t i", t=PACK, c=P // run, i=run),
+            in_=in_.rearrange("p (g c i t) -> p g c t i", t=PACK, c=P // run, i=run),
+        )
 
     with ExitStack() as ctx:
         lists = ctx.enter_context(tc.tile_pool(name="lists", bufs=1))
@@ -87,6 +90,13 @@ def tile_list_reindeer_route_features_kernel(
         w2_plane = sbuf("w2_plane", [P, H], U8)
         for plane in (tab2_plane, w2_plane):
             nc.vector.memset(plane[:].bitcast(I32), 0)
+        pages = [sbuf("page%d" % s, [P, S], F32) for s in range(GROUPS * PACK)]
+
+        def clear_pages(first, last):
+            for page in pages[first:last]:
+                nc.vector.memset(page[:], 0.0)
+
+        clear_pages(0, 5)
         identity = sbuf("identity", [P, P], F32)
         make_identity(nc, identity[:])
         warm = sbuf("warm", [P, 1], F32)
@@ -139,29 +149,19 @@ def tile_list_reindeer_route_features_kernel(
 
         w2_codes = sbuf("w2_codes", [P, 2 * H], U8)
         w2_dealt_plane = sbuf("w2_dealt_plane", [P, H], U8)
-        nc.vector.tensor_copy(
-            out=w2_codes[:].rearrange("p (g t m b) -> p g m t b", g=GROUPS, t=PACK, b=2),
-            in_=w2_raw[:].rearrange("p (g m t b) -> p g m t b", g=GROUPS, t=PACK, b=2),
-        )
-        nc.vector.tensor_copy(
-            out=w2_dealt_plane[:].rearrange("p (g t m) -> p g m t", g=GROUPS, t=PACK),
-            in_=w2_plane[:].rearrange("p (g m t) -> p g m t", g=GROUPS, t=PACK),
-        )
-
+        for g in range(GROUPS):
+            group_bytes = slice(2 * GROUP * g, 2 * GROUP * (g + 1))
+            nc.vector.tensor_copy(
+                out=w2_codes[:, group_bytes].rearrange("p (t c i b) -> p c t i b", t=PACK, i=8, b=2),
+                in_=w2_raw[:, group_bytes].rearrange("p (c i t b) -> p c t i b", t=PACK, i=8, b=2),
+            )
+        clear_pages(5, 6)
         v2_plane = sbuf("v2_plane", [P, L], U8)
         v2_codes = sbuf("v2_codes", [P, L], U32)
-        nc.vector.tensor_copy(v2_plane[:], tab2_plane[:].indirect(idx2[:]))
         nc.vector.tensor_copy(v2_codes[:], tab2_all[:].indirect(idx2[:]))
-
-        pages = {}
-
-        def clear_page(s, engine):
-            pages[s] = sbuf("page%d" % s, [P, S], F32)
-            engine.memset(pages[s][:], 0.0)
-
-        for s in range(3):
-            clear_page(s, nc.vector)
-        clear_page(3, nc.gpsimd)
+        nc.vector.tensor_copy(v2_plane[:], tab2_plane[:].indirect(idx2[:]))
+        deal_columns(w2_dealt_plane[:], w2_plane[:], 16)
+        clear_pages(6, 8)
 
         def load_w4(a, g):
             return load_weight("w4_raw%d%d" % (a, g), w4[a * GROUP : (a + 1) * GROUP, :], g)
@@ -171,8 +171,10 @@ def tile_list_reindeer_route_features_kernel(
         tab_all = sbuf("tab_all", [P, T], U32)
         nc.sync.dma_start(out=tab_all[:].bitcast(I32), in_=packed_words(tab_words[0]))
         tab_plane = sbuf("tab_plane", [P, T], U8)
-        nc.gpsimd.memset(tab_plane[:].bitcast(I32), 0)
-        load_scale_rows([nc.sync] * 4, tab_plane, tab_scales)
+        w3_plane = sbuf("w3_plane", [P, H], U8)
+        for plane, scales in ((tab_plane, tab_scales), (w3_plane, w3_scales)):
+            nc.vector.memset(plane[:].bitcast(I32), 0)
+            load_scale_rows([nc.sync] * 4, plane, scales)
 
         def place_rumen(s):
             g, t = slots[s]
@@ -189,8 +191,6 @@ def tile_list_reindeer_route_features_kernel(
 
         for s in range(5):
             place_rumen(s)
-            if s < 4:
-                clear_page(s + 4, nc.gpsimd)
 
         def round_weight(raw, rounded):
             nc.scalar.copy(
@@ -239,11 +239,8 @@ def tile_list_reindeer_route_features_kernel(
         round_w4(1)
 
         w3_raw = sbuf("w3_raw", [P, GROUPS, H], U32)
-        w3_plane = sbuf("w3_plane", [P, H], U8)
-        nc.gpsimd.memset(w3_plane[:].bitcast(I32), 0)
         for a in range(GROUPS):
             nc.sync.dma_start(out=w3_raw[:, a, :].bitcast(I32), in_=packed_words(w3_words[a]))
-        load_scale_rows([nc.sync] * 4, w3_plane, w3_scales)
 
         def track_features(g, h):
             for t in range(PACK):
@@ -314,14 +311,9 @@ def tile_list_reindeer_route_features_kernel(
 
         w3_codes = sbuf("w3_codes", [P, GROUPS, H], U32)
         w3_dealt_plane = sbuf("w3_dealt_plane", [P, H], U8)
-        nc.vector.tensor_copy(
-            out=w3_codes[:].bitcast(I32).rearrange("p a (g t m) -> p (a g) m t", g=GROUPS, t=PACK),
-            in_=w3_raw[:].bitcast(I32).rearrange("p a (g m t) -> p (a g) m t", g=GROUPS, t=PACK),
-        )
-        nc.vector.tensor_copy(
-            out=w3_dealt_plane[:].rearrange("p (g t m) -> p g m t", g=GROUPS, t=PACK),
-            in_=w3_plane[:].rearrange("p (g m t) -> p g m t", g=GROUPS, t=PACK),
-        )
+        deal_columns(w3_codes[:].rearrange("p a c -> p (a c)").bitcast(I32),
+                     w3_raw[:].rearrange("p a c -> p (a c)").bitcast(I32), 4)
+        deal_columns(w3_dealt_plane[:], w3_plane[:], 16)
 
         def interleave(copy, out, in_):
             copy(
@@ -335,13 +327,13 @@ def tile_list_reindeer_route_features_kernel(
             per_bank = BANK // width
             for first_slot in range(0, PACK, per_bank):
                 sums = bank(tag, [P, per_bank, width])
-                for e in range(per_bank):
-                    for a in range(GROUPS):
+                for a in range(GROUPS):
+                    for e in range(per_bank):
                         codes, plane = weights(a, g, first_slot + e)
                         nc.tensor.matmul_mx(
                             out=sums[:, e, :], lhsT=codes.bitcast(FP8X4), lhsT_scale=plane,
                             rhs=moving[a][0][:].bitcast(FP8X4), rhs_scale=moving[a][1][:],
-                            start=(a == 0), stop=(a == GROUPS - 1),
+                            start=(a, e) == (0, 0), stop=(a, e) == (GROUPS - 1, per_bank - 1),
                         )
                 empty(slice(first_slot, first_slot + per_bank), sums[:])
 
@@ -372,7 +364,7 @@ def tile_list_reindeer_route_features_kernel(
             first, width = CHUNKS[c]
             cols = slice(first, first + width)
             y = sbuf("y", [P, PACK, width], F32, bufs=3)
-            products("outer", g, width, w4_slot, x_mx,
+            products("turn" if (c, g) == (len(CHUNKS) - 1, 1) else "outer", g, width, w4_slot, x_mx,
                      lambda held, sums: nc.scalar.copy(out=y[:, held, :], in_=sums))
             nc.sync.dma_start(
                 out=out_0[g * GROUP : (g + 1) * GROUP, cols].rearrange("(p t) j -> p t j", t=PACK), in_=y[:])

@@ -36,6 +36,8 @@ ROOMS = {
     "tab2_plane": 31,
     "w4_raw10": 32, "track01": 32,
     "tab2_all": 40, "tab_all": 40, "squashed": 40, "x_planar": 52,
+    "page3": 88, "w2_plane": 91.5, "w3_plane": 92,
+    "rumen0": 93, "page4": 93, "rumen1": 97, "page5": 97, "rumen2": 101, "page6": 101, "rumen3": 105, "page7": 105,
     "w1_codes0": 56, "rumen5": 56, "w1_plane0": 58, "rumen6": 58,
     "v_codes0": 60, "rumen7": 60, "w4_codes": 60,
     "minus_wgs3": 68, "w3_codes": 68,
@@ -76,7 +78,7 @@ def tile_list_reindeer_route_features_kernel(
         def sbuf(name, shape, dtype, bufs=1):
             if name in ROOMS:
                 return turns.tile(shape, dtype, name=name, tag=name, bufs=bufs, align_bytes=ALIGN,
-                                  offset=ROOMS[name] * KIB)
+                                  offset=int(ROOMS[name] * KIB))
             return keep.tile(shape, dtype, name=name, tag=name, bufs=bufs, align_bytes=ALIGN)
 
         def bank(tag, shape):
@@ -92,11 +94,11 @@ def tile_list_reindeer_route_features_kernel(
             nc.vector.memset(plane[:].bitcast(I32), 0)
         pages = [sbuf("page%d" % s, [P, S], F32) for s in range(GROUPS * PACK)]
 
-        def clear_pages(first, last):
-            for page in pages[first:last]:
-                nc.vector.memset(page[:], 0.0)
+        def clear(engine, tile):
+            engine.memset(tile[:].bitcast(I32), 0)
 
-        clear_pages(0, 5)
+        for s in range(2):
+            clear(nc.vector, pages[s])
         identity = sbuf("identity", [P, P], F32)
         make_identity(nc, identity[:])
         warm = sbuf("warm", [P, 1], F32)
@@ -155,13 +157,13 @@ def tile_list_reindeer_route_features_kernel(
                 out=w2_codes[:, group_bytes].rearrange("p (t c i b) -> p c t i b", t=PACK, i=8, b=2),
                 in_=w2_raw[:, group_bytes].rearrange("p (c i t b) -> p c t i b", t=PACK, i=8, b=2),
             )
-        clear_pages(5, 6)
+        clear(nc.vector, pages[2])
         v2_plane = sbuf("v2_plane", [P, L], U8)
         v2_codes = sbuf("v2_codes", [P, L], U32)
         nc.vector.tensor_copy(v2_codes[:], tab2_all[:].indirect(idx2[:]))
         nc.vector.tensor_copy(v2_plane[:], tab2_plane[:].indirect(idx2[:]))
         deal_columns(w2_dealt_plane[:], w2_plane[:], 16)
-        clear_pages(6, 8)
+        clear(nc.gpsimd, pages[3])
 
         def load_w4(a, g):
             return load_weight("w4_raw%d%d" % (a, g), w4[a * GROUP : (a + 1) * GROUP, :], g)
@@ -173,7 +175,7 @@ def tile_list_reindeer_route_features_kernel(
         tab_plane = sbuf("tab_plane", [P, T], U8)
         w3_plane = sbuf("w3_plane", [P, H], U8)
         for plane, scales in ((tab_plane, tab_scales), (w3_plane, w3_scales)):
-            nc.vector.memset(plane[:].bitcast(I32), 0)
+            clear(nc.gpsimd, plane)
             load_scale_rows([nc.sync] * 4, plane, scales)
 
         def place_rumen(s):
@@ -191,6 +193,8 @@ def tile_list_reindeer_route_features_kernel(
 
         for s in range(5):
             place_rumen(s)
+            if s < 4:
+                clear(nc.gpsimd, pages[s + 4])
 
         def round_weight(raw, rounded):
             nc.scalar.copy(

from contextlib import ExitStack

import concourse.mybir as mybir
from concourse.masks import make_identity

K, T, S, T2, L, H, N = 512, 4096, 1024, 2048, 512, 1024, 1024
FLOPS = 2 * (K * H * S + K * H * L + H * H * S + H * N * S)

F32 = mybir.dt.float32
BF16 = mybir.dt.bfloat16
I32 = mybir.dt.int32
U32 = mybir.dt.uint32
U16 = mybir.dt.uint16
U8 = mybir.dt.uint8
FP8X4 = mybir.dt.float8_e4m3fn_x4
FP4X4 = mybir.dt.float4_e2m1fn_x4
MULT = mybir.AluOpType.mult
ADD = mybir.AluOpType.add
ACT = mybir.ActivationFunctionType

P = 128
PACK = 4
GROUP = P * PACK
GROUPS = H // GROUP
BANK = 512
HALF = 512
CHUNK_WIDTHS = (256, 256, 256, 256)
CHUNKS = [(sum(CHUNK_WIDTHS[:c]), width) for c, width in enumerate(CHUNK_WIDTHS)]
ALIGN = 64
KIB = 1024
ROOMS = {
    "w1_raw0": 0, "w4_raw01": 0, "track10": 0,
    "w2_raw": 7,
    "w1_raw1": 8, "track11": 8, "w4_raw11": 12, "w3_raw": 16,
    "w4_raw00": 24, "track00": 24,
    "tab2_plane": 31,
    "w4_raw10": 32, "track01": 32,
    "tab2_all": 40, "tab_all": 40, "squashed": 40, "x_planar": 52,
    "page3": 88, "w2_plane": 91.5, "w3_plane": 92,
    "rumen0": 93, "page4": 93, "rumen1": 97, "page5": 97, "rumen2": 101, "page6": 101, "rumen3": 105, "page7": 105,
    "w1_codes0": 56, "rumen5": 56, "w1_plane0": 58, "rumen6": 58,
    "v_codes0": 60, "rumen7": 60, "w4_codes": 60,
    "minus_wgs3": 68, "w3_codes": 68,
    "w1_rounded": 76, "z_pairs": 76,
    "spread": 84, "tab_plane": 84, "z_rounded": 84,
}


def tile_list_reindeer_route_features_kernel(
    tc, tab_words, tab_scales, offs, tab2_words, tab2_scales, offs2, pos1, w1, terrain,
    w2_words, w2_scales, bias, wgs, w3_words, w3_scales, gain, w4, out_0, out_1, out_2,
):
    nc = tc.nc

    def load_scale_rows(queues, plane, scales):
        passes = scales.shape[0]
        for q, queue in enumerate(queues):
            queue.dma_start(
                out=plane[32 * q : 32 * q + 4 * passes, :].bitcast(I32),
                in_=scales[:, 4 * q : 4 * q + 4, :].bitcast(I32),
            )

    def packed_words(words):
        return words.rearrange("p c i -> p (c i)").bitcast(I32)

    def deal_columns(out, in_, run):
        nc.vector.tensor_copy(
            out=out.rearrange("p (g t c i) -> p g c t i", t=PACK, c=P // run, i=run),
            in_=in_.rearrange("p (g c i t) -> p g c t i", t=PACK, c=P // run, i=run),
        )

    with ExitStack() as ctx:
        lists = ctx.enter_context(tc.tile_pool(name="lists", bufs=1))
        keep = ctx.enter_context(tc.tile_pool(name="keep", bufs=1))
        turns = ctx.enter_context(tc.tile_pool(name="turns", bufs=1))
        psum = ctx.enter_context(tc.psum_pool(name="psum", bufs=1))

        def sbuf(name, shape, dtype, bufs=1):
            if name in ROOMS:
                return turns.tile(shape, dtype, name=name, tag=name, bufs=bufs, align_bytes=ALIGN,
                                  offset=int(ROOMS[name] * KIB))
            return keep.tile(shape, dtype, name=name, tag=name, bufs=bufs, align_bytes=ALIGN)

        def bank(tag, shape):
            return psum.tile(shape, F32, name=tag, tag=tag, bufs={"sums": 3, "turn": 3, "outer": 2}[tag])

        idx2 = lists.tile([P, L // 16], U16, name="idx2")
        place = lists.tile([P, L // 16], U16, name="place")
        idx = lists.tile([P, S // 16], U16, name="idx")

        tab2_plane = sbuf("tab2_plane", [P, T2], U8)
        w2_plane = sbuf("w2_plane", [P, H], U8)
        for plane in (tab2_plane, w2_plane):
            nc.vector.memset(plane[:].bitcast(I32), 0)
        pages = [sbuf("page%d" % s, [P, S], F32) for s in range(GROUPS * PACK)]

        def clear(engine, tile):
            engine.memset(tile[:].bitcast(I32), 0)

        for s in range(2):
            clear(nc.vector, pages[s])
        identity = sbuf("identity", [P, P], F32)
        make_identity(nc, identity[:])
        warm = sbuf("warm", [P, 1], F32)
        nc.scalar.activation(out=warm[:], in_=identity[:, 0:1], func=ACT.Tanh)

        slots = [(g, t) for g in range(GROUPS) for t in range(PACK)]

        wgs_rows = sbuf("wgs_rows", [P, L], F32)
        w2_raw = sbuf("w2_raw", [P, 2 * H], U8)
        tab2_all = sbuf("tab2_all", [P, T2], U32)
        bias_col = sbuf("bias_col", [P, GROUPS, PACK], F32)
        gain_col = sbuf("gain_col", [P, GROUPS, PACK], F32)

        nc.sync.dma_start(idx2[:], offs2)
        nc.sync.dma_start(out=bias_col[:], in_=bias.rearrange("(g p t) -> p g t", p=P, t=PACK))
        nc.sync.dma_start(place[:], pos1)
        nc.sync.dma_start(idx[:], offs)
        nc.sync.dma_start(out=wgs_rows[:], in_=wgs)
        nc.sync.dma_start(out=w2_raw[:].bitcast(I32), in_=w2_words[0].bitcast(I32))
        nc.sync.dma_start(out=gain_col[:], in_=gain.rearrange("(g p t) -> p g t", p=P, t=PACK))
        nc.sync.dma_start(out=tab2_all[:].bitcast(I32), in_=packed_words(tab2_words[0]))
        load_scale_rows([nc.sync] * 4, tab2_plane, tab2_scales)
        load_scale_rows([nc.sync] * 4, w2_plane, w2_scales)

        def load_weight(name, weight_rows, g):
            raw = sbuf(name, [P, PACK, GROUP], F32)
            nc.sync.dma_start(
                out=raw[:],
                in_=weight_rows[:, g * GROUP : (g + 1) * GROUP].rearrange("(p j) c -> p j c", j=PACK),
            )
            return raw

        turned = bank("turn", [P, L // P, P])
        for jb in range(L // P):
            nc.tensor.transpose(turned[:, jb, :], wgs_rows[:, jb * P : (jb + 1) * P], identity[:])
        minus_wgs = []
        for t in range(PACK):
            spread = sbuf("spread", [P, L // P, 4, 32], F32, bufs=2)
            nc.scalar.activation(
                out=spread[:],
                in_=turned[:].rearrange("j b (c t) -> j b t c", t=PACK)[:, :, t : t + 1, :].to_broadcast(
                    [P, L // P, 4, 32]),
                func=ACT.Copy, scale=-1.0,
            )
            back = bank("turn", [P, L // P, P])
            for jb in range(L // P):
                nc.tensor.transpose(back[:, jb, :], spread[:, jb, :, :].rearrange("j q c -> j (q c)"), identity[:])
            minus_wgs.append(sbuf("minus_wgs%d" % t, [P, L], F32))
            nc.scalar.copy(out=minus_wgs[t][:], in_=back[:].rearrange("p b j -> p (b j)"))

        w2_codes = sbuf("w2_codes", [P, 2 * H], U8)
        w2_dealt_plane = sbuf("w2_dealt_plane", [P, H], U8)
        for g in range(GROUPS):
            group_bytes = slice(2 * GROUP * g, 2 * GROUP * (g + 1))
            nc.vector.tensor_copy(
                out=w2_codes[:, group_bytes].rearrange("p (t c i b) -> p c t i b", t=PACK, i=8, b=2),
                in_=w2_raw[:, group_bytes].rearrange("p (c i t b) -> p c t i b", t=PACK, i=8, b=2),
            )
        clear(nc.vector, pages[2])
        v2_plane = sbuf("v2_plane", [P, L], U8)
        v2_codes = sbuf("v2_codes", [P, L], U32)
        nc.vector.tensor_copy(v2_codes[:], tab2_all[:].indirect(idx2[:]))
        nc.vector.tensor_copy(v2_plane[:], tab2_plane[:].indirect(idx2[:]))
        deal_columns(w2_dealt_plane[:], w2_plane[:], 16)
        clear(nc.gpsimd, pages[3])

        def load_w4(a, g):
            return load_weight("w4_raw%d%d" % (a, g), w4[a * GROUP : (a + 1) * GROUP, :], g)

        w1_raw = [load_weight("w1_raw%d" % g, w1, g) for g in range(GROUPS)]
        w4_raw = {(a, 0): load_w4(a, 0) for a in range(GROUPS)}
        tab_all = sbuf("tab_all", [P, T], U32)
        nc.sync.dma_start(out=tab_all[:].bitcast(I32), in_=packed_words(tab_words[0]))
        tab_plane = sbuf("tab_plane", [P, T], U8)
        w3_plane = sbuf("w3_plane", [P, H], U8)
        for plane, scales in ((tab_plane, tab_scales), (w3_plane, w3_scales)):
            clear(nc.gpsimd, plane)
            load_scale_rows([nc.sync] * 4, plane, scales)

        def place_rumen(s):
            g, t = slots[s]
            sums = bank("outer", [P, L])
            nc.tensor.matmul_mx(
                out=sums[:],
                lhsT=w2_codes[:, 2 * P * s : 2 * P * (s + 1)].bitcast(FP4X4),
                lhsT_scale=w2_dealt_plane[:, P * s : P * (s + 1)],
                rhs=v2_codes[:].bitcast(FP8X4), rhs_scale=v2_plane[:], start=True, stop=True,
            )
            rumen = sbuf("rumen%d" % s, [P, L], F32)
            nc.scalar.activation(out=rumen[:], in_=sums[:], func=ACT.Identity, bias=bias_col[:, g, t : t + 1])
            nc.vector.tensor_tensor(pages[s][:].indirect(place[:]), rumen[:], minus_wgs[t][:], MULT)

        for s in range(5):
            place_rumen(s)
            if s < 4:
                clear(nc.gpsimd, pages[s + 4])

        def round_weight(raw, rounded):
            nc.scalar.copy(
                out=rounded[:].rearrange("p (t m) j -> p m j t", t=PACK),
                in_=raw[:].rearrange("p j (m t) -> p m j t", t=PACK),
            )

        w1_mx = []
        for g in range(GROUPS):
            rounded = sbuf("w1_rounded", [P, GROUP, PACK], BF16, bufs=2)
            round_weight(w1_raw[g], rounded)
            codes = sbuf("w1_codes%d" % g, [P, GROUP], U32)
            plane = sbuf("w1_plane%d" % g, [P, GROUP], U8)
            nc.vector.quantize_mx(out=codes[:].bitcast(FP8X4), scales=plane[:],
                                  in_=rounded[:].rearrange("p c j -> p (c j)"))
            w1_mx.append((codes, plane))

        v_mx = []
        for h in range(S // HALF):
            picked = idx[:, h * HALF // 16 : (h + 1) * HALF // 16]
            codes = sbuf("v_codes%d" % h, [P, HALF], U32)
            plane = sbuf("v_plane%d" % h, [P, HALF], U8)
            nc.vector.tensor_copy(plane[:], tab_plane[:].indirect(picked))
            nc.vector.tensor_copy(codes[:], tab_all[:].indirect(picked))
            v_mx.append((codes, plane))

        w4_rounded = {}

        def round_w4(g):
            for a in range(GROUPS):
                w4_rounded[a, g] = sbuf("w4_rounded%d%d" % (a, g), [P, GROUP, PACK], BF16)
                round_weight(w4_raw[a, g], w4_rounded[a, g])

        for a in range(GROUPS):
            w4_raw[a, 1] = load_w4(a, 1)
        round_w4(0)
        track = {}
        for g in range(GROUPS):
            for h in range(S // HALF):
                track[g, h] = sbuf("track%d%d" % (g, h), [P, PACK, HALF], F32)
                nc.sync.dma_start(
                    out=track[g, h][:],
                    in_=terrain[g * GROUP : (g + 1) * GROUP, h * HALF : (h + 1) * HALF].rearrange(
                        "(p t) j -> p t j", t=PACK),
                )
        round_w4(1)

        w3_raw = sbuf("w3_raw", [P, GROUPS, H], U32)
        for a in range(GROUPS):
            nc.sync.dma_start(out=w3_raw[:, a, :].bitcast(I32), in_=packed_words(w3_words[a]))

        def track_features(g, h):
            for t in range(PACK):
                sums = bank("sums", [P, HALF])
                nc.tensor.matmul_mx(
                    out=sums[:],
                    lhsT=w1_mx[g][0][:, t * P : (t + 1) * P].bitcast(FP8X4),
                    lhsT_scale=w1_mx[g][1][:, t * P : (t + 1) * P],
                    rhs=v_mx[h][0][:].bitcast(FP8X4), rhs_scale=v_mx[h][1][:], start=True, stop=True,
                )
                nc.vector.tensor_tensor(track[g, h][:, t, :], sums[:], track[g, h][:, t, :], MULT)

        def track_columns(g, t, first, count):
            h, inside = divmod(first, HALF)
            return track[g, h][:, t, inside : inside + count]

        def quantise(rounded, width, name, bufs):
            codes = sbuf(name + "_codes", [P, width], U32, bufs=bufs)
            plane = sbuf(name + "_plane", [P, width], U8, bufs=bufs)
            nc.vector.quantize_mx(out=codes[:].bitcast(FP8X4), scales=plane[:], in_=rounded)
            return codes, plane

        def turned_pairs(g, u, c):
            first, width = CHUNKS[c]
            blocks = width // P
            turned = bank("turn", [P, blocks, 2, P])
            terms = []
            for source in ("track", "page"):
                for b in range(blocks):
                    for e in range(2):
                        t, start = 2 * u + e, first + b * P
                        if source == "track":
                            terms.append((turned[:, b, e, :], track_columns(g, t, start, P)))
                        else:
                            terms.append((turned[:, b, e, :], pages[PACK * g + t][:, start : start + P]))
            for i, (out, term) in enumerate(terms):
                nc.tensor.matmul(out, lhsT=term, rhs=identity[:], is_transpose=True,
                                 start=(i == 0), stop=(i == len(terms) - 1))
            pairs = sbuf("z_pairs", [P, blocks, P, 2], BF16, bufs=6)
            nc.scalar.copy(out=pairs[:], in_=turned[:].rearrange("j b e p -> j b p e"))
            return pairs

        def difference(c, pairs):
            width = CHUNKS[c][1]
            blocks = width // P
            back = bank("turn", [P, blocks, 2, P])
            for b in range(blocks):
                for u in range(2):
                    words = pairs[u][:, b, :, :].rearrange("j p e -> j (p e)").bitcast(F32)
                    nc.tensor.transpose(back[:, b, u, :], words, identity[:])
            rounded = sbuf("z_rounded", [P, width * PACK], BF16, bufs=2)
            nc.scalar.copy(
                out=rounded[:].bitcast(F32).rearrange("p (b j u) -> p b j u", b=blocks, u=2),
                in_=back[:].rearrange("p b u j -> p b j u"),
            )
            return quantise(rounded[:], width, "z", GROUPS * len(CHUNKS))

        z_mx = {}
        for h in range(S // HALF):
            track_features(0, h)
        place_rumen(5)
        place_rumen(6)
        for c in range(len(CHUNKS)):
            z_mx[0, c] = difference(c, [turned_pairs(0, u, c) for u in range(2)])
        track_features(1, 0)
        place_rumen(7)
        low_pairs = {c: turned_pairs(1, 0, c) for c in range(2)}

        w3_codes = sbuf("w3_codes", [P, GROUPS, H], U32)
        w3_dealt_plane = sbuf("w3_dealt_plane", [P, H], U8)
        deal_columns(w3_codes[:].rearrange("p a c -> p (a c)").bitcast(I32),
                     w3_raw[:].rearrange("p a c -> p (a c)").bitcast(I32), 4)
        deal_columns(w3_dealt_plane[:], w3_plane[:], 16)

        def interleave(copy, out, in_):
            copy(
                out=out.rearrange("p (c i t) -> p c t i", i=4, t=PACK),
                in_=in_.rearrange("p t (c i) -> p c t i", i=4),
            )

        y_plane = sbuf("y_plane", [P, GROUPS, S], U8)

        def products(tag, g, width, weights, moving, empty):
            per_bank = BANK // width
            for first_slot in range(0, PACK, per_bank):
                sums = bank(tag, [P, per_bank, width])
                for a in range(GROUPS):
                    for e in range(per_bank):
                        codes, plane = weights(a, g, first_slot + e)
                        nc.tensor.matmul_mx(
                            out=sums[:, e, :], lhsT=codes.bitcast(FP8X4), lhsT_scale=plane,
                            rhs=moving[a][0][:].bitcast(FP8X4), rhs_scale=moving[a][1][:],
                            start=(a, e) == (0, 0), stop=(a, e) == (GROUPS - 1, per_bank - 1),
                        )
                empty(slice(first_slot, first_slot + per_bank), sums[:])

        def w3_slot(a, g, t):
            cols = slice((PACK * g + t) * P, (PACK * g + t + 1) * P)
            return w3_codes[:, a, cols], w3_dealt_plane[4 * a : P, cols]

        def w4_slot(a, g, t):
            cols = slice(t * P, (t + 1) * P)
            return w4_codes[:, GROUPS * a + g, cols], w4_plane[:, GROUPS * a + g, cols]

        def bounded(g, c):
            first, width = CHUNKS[c]
            squashed = sbuf("squashed", [P, PACK, width], F32, bufs=3)
            products("sums", g, width, w3_slot, [z_mx[a, c] for a in range(GROUPS)],
                     lambda held, sums: nc.scalar.activation(out=squashed[:, held, :], in_=sums, func=ACT.Tanh))
            planar = sbuf("x_planar", [P, PACK, width], BF16, bufs=2)
            for t in range(PACK):
                nc.vector.scalar_tensor_tensor(
                    out=planar[:, t, :], in0=squashed[:, t, :], scalar=gain_col[:, g, t : t + 1],
                    in1=track_columns(g, t, first, width), op0=MULT, op1=ADD,
                )
            rounded = sbuf("x_rounded", [P, width * PACK], BF16, bufs=2)
            interleave(nc.vector.tensor_copy, rounded[:], planar[:])
            return quantise(rounded[:], width, "x", 4)

        def result(g, c, x_mx):
            first, width = CHUNKS[c]
            cols = slice(first, first + width)
            y = sbuf("y", [P, PACK, width], F32, bufs=3)
            products("turn" if (c, g) == (len(CHUNKS) - 1, 1) else "outer", g, width, w4_slot, x_mx,
                     lambda held, sums: nc.scalar.copy(out=y[:, held, :], in_=sums))
            nc.sync.dma_start(
                out=out_0[g * GROUP : (g + 1) * GROUP, cols].rearrange("(p t) j -> p t j", t=PACK), in_=y[:])
            rounded = sbuf("y_rounded", [P, width * PACK], BF16, bufs=2)
            interleave(nc.vector.tensor_copy, rounded[:], y[:])
            codes = sbuf("y_codes", [P, width], U32, bufs=3)
            nc.vector.quantize_mx(out=codes[:].bitcast(FP8X4), scales=y_plane[:, g, cols], in_=rounded[:])
            nc.sync.dma_start(out=packed_words(out_1[g])[:, cols], in_=codes[:].bitcast(I32))

        def store_scale_rows(cols):
            for q in range(4):
                nc.sync.dma_start(
                    out=out_2[:, 4 * q : 4 * q + 4, cols].rearrange("g r j -> r g j").bitcast(I32),
                    in_=y_plane[32 * q : 32 * q + 4, :, cols].bitcast(I32),
                )

        w4_codes = sbuf("w4_codes", [P, GROUPS * GROUPS, GROUP], U32)
        w4_plane = sbuf("w4_plane", [P, GROUPS * GROUPS, GROUP], U8)

        x_mx = {}
        for step in range(len(CHUNKS) + 2):
            if step < len(CHUNKS):
                low = low_pairs[step] if step in low_pairs else turned_pairs(1, 0, step)
                z_mx[1, step] = difference(step, [low, turned_pairs(1, 1, step)])
            if 1 <= step <= len(CHUNKS):
                x_mx[step - 1] = [bounded(g, step - 1) for g in range(GROUPS)]
            if step >= 2:
                for g in range(GROUPS):
                    result(g, step - 2, x_mx[step - 2])
            if step == len(CHUNKS):
                store_scale_rows(slice(0, CHUNKS[-1][0]))
            if step == 0:
                track_features(1, 1)
                for (a, g), rounded in w4_rounded.items():
                    nc.vector.quantize_mx(
                        out=w4_codes[:, GROUPS * a + g, :].bitcast(FP8X4), scales=w4_plane[:, GROUPS * a + g, :],
                        in_=rounded[:].rearrange("p c j -> p (c j)"))

        store_scale_rows(slice(CHUNKS[-1][0], S))
